import numpy as np, ml_dtypes
CORES = [16,32,48,64,80]
N = 5
NH, QP = 5, 32
def setup_inputs(rng):
    return {"q": rng.standard_normal((N, 128, NH * QP), dtype=np.float32).astype(ml_dtypes.bfloat16), "k": rng.standard_normal((N, 128, NH * 128), dtype=np.float32).astype(ml_dtypes.bfloat16), "v": rng.standard_normal((N, 128, NH * 128), dtype=np.float32).astype(ml_dtypes.bfloat16)}
def setup_inputs_big(rng):
    d = setup_inputs(rng)
    for k in ("q", "k", "v"): d[k] = (d[k].astype(np.float32) * 1024.0).astype(d[k].dtype)
    return d
def setup_inputs_small(rng):
    d = setup_inputs(rng)
    for k in ("q", "k", "v"): d[k] = (d[k].astype(np.float32) * (1 / 1024.0)).astype(d[k].dtype)
    return d
def setup_inputs_apart(rng):
    d = setup_inputs(rng)
    f = (10.0 ** rng.permutation(np.linspace(-1.5, 1.5, N))).astype(np.float32).reshape(N, 1, 1)
    for k in ("q", "k", "v"): d[k] = (d[k].astype(np.float32) * f).astype(d[k].dtype)
    return d
def reference(q, k, v):
    Q, K, V = q.astype(np.float64), k.astype(np.float64), v.astype(np.float64)
    y = np.zeros((N, 128, NH * QP))
    for r in range(N):
        for h in range(NH):
            for j in range(N):
                S = np.maximum(K[j][:, 128 * h:128 * h + 128].T @ Q[r][:, QP * h:QP * h + QP], 0.0)
                y[r][:, QP * h:QP * h + QP] += V[j][:, 128 * h:128 * h + 128].T @ S
    return {"y": y.astype(ml_dtypes.bfloat16 if q.dtype != np.float64 else np.float64)}

@@ -1,0 +1,104 @@
+from concourse.bass import DstId, RemoteDMATransfer
+from concourse.mybir import AluOpType
+
+N, NH, QP, KP = 5, 5, 32, 128
+W = NH * QP
+
+SCRATCH = {
+    "ks": ("sbuf", [128, NH * KP], "bfloat16"),
+    "vs": ("sbuf", [128, NH * KP], "bfloat16"),
+    "zero": ("sbuf", [128, W], "float32"),
+    "ybuf": ("sbuf", [128, W], "bfloat16"),
+    "ps0": ("psum", [128, 512], "float32"),
+    "ps1": ("psum", [128, 512], "float32"),
+    "pacc": ("psum", [128, 512], "float32"),
+}
+SEMAPHORES = ["qld", "kld", "vld", "zf", "sm", "rl", "om", "ad", "sent", "st"]
+for _j in range(N):
+    SCRATCH["ql%d" % _j] = ("sbuf", [128, W], "bfloat16")
+    SCRATCH["ol%d" % _j] = ("sbuf", [128, W], "bfloat16")
+    SCRATCH["sb%d" % _j] = ("sbuf", [128, W], "bfloat16")
+    SCRATCH["ob%d" % _j] = ("sbuf", [128, W], "bfloat16")
+    SCRATCH["po%d" % _j] = ("psum", [128, 512], "float32")
+    SEMAPHORES += ["qa%d" % _j, "oa%d" % _j, "cp%d" % _j]
+
+
+def rank_program(g, core, T, topo):
+    r = T.rank_of(core)
+    if r is None:
+        return
+    cores, sem = T.cores, T.sem
+    n = len(cores)
+    after = [(r + d) % n for d in range(1, n)]
+    items = [r] + [(r - d) % n for d in range(1, n)]
+    mask = topo.mask(core, cores[after[0]])
+    for j in after:
+        mask &= topo.mask(core, cores[j])
+    ne = bin(mask).count("1")
+    myq = T["ql%d" % r]
+
+    g.sync.dma_start(myq[:], T.q[:]).then_inc(sem.qld, 16)
+    g.sync.dma_start(T.ks[:], T.k[:]).then_inc(sem.kld, 16)
+    g.scalar.wait_ge(sem.qld, 16)
+    g.scalar.dma_start(T.vs[:], T.v[:]).then_inc(sem.vld, 16)
+    g.vector.memset(T.zero[:], 0.0).then_inc(sem.zf, 1)
+
+    g.wait_ge(sem.qld, 16)
+    ids = []
+    for j in after:
+        rid, pid, _se = topo.addr(cores[j])
+        ids.append(DstId(rid=rid, pnc=pid))
+    g.remote_dma_fused(
+        [RemoteDMATransfer(dst_ids=ids, dma_engine_mask=mask, remote_sem=sem["qa%d" % r],
+                           srcs=[myq[:]], dsts=[myq[:] for _ in after], alu_op=0)],
+        local_sem=sem.sent)
+    for i in range(1, n):
+        j = items[i]
+        rid, pid, _se = topo.addr(cores[j])
+        g.wait_ge(sem["cp%d" % i], 1)
+        g.remote_dma(T["ol%d" % r][:], T["ob%d" % i][:], sem["oa%d" % r], sem.sent, pid, rid, mask)
+    g.wait_ge(sem.sent, ne * n)
+
+    for i, j in enumerate(items):
+        if i == 0:
+            g.tensor.wait_ge(sem.qld, 16)
+            g.tensor.wait_ge(sem.kld, 16)
+        else:
+            g.tensor.wait_ge(sem["qa%d" % j], ne)
+        ps, qj = T["ps%d" % (i % 2)], T["ql%d" % j]
+        for h in range(NH):
+            g.tensor.matmul(ps[:, h * QP:(h + 1) * QP], T.ks[:, h * KP:(h + 1) * KP],
+                            qj[:, h * QP:(h + 1) * QP], True, True).then_inc(sem.sm, 1)
+        if i == 0:
+            g.tensor.wait_ge(sem.vld, 16)
+        g.tensor.wait_ge(sem.rl, i + 1)
+        po, sb = T["po%d" % i], T["sb%d" % i]
+        for h in range(NH):
+            g.tensor.matmul(po[:, h * QP:(h + 1) * QP], T.vs[:, h * KP:(h + 1) * KP],
+                            sb[:, h * QP:(h + 1) * QP], True, True).then_inc(sem.om, 1)
+
+    g.vector.wait_ge(sem.zf, 1)
+    for i in range(n):
+        g.vector.wait_ge(sem.sm, NH * (i + 1))
+        g.vector.tensor_tensor(T["sb%d" % i][:], T["ps%d" % (i % 2)][:, 0:W], T.zero[:],
+                               AluOpType.max).then_inc(sem.rl, 1)
+        if i > 0:
+            g.vector.wait_ge(sem.om, NH * (i + 1))
+            g.vector.tensor_copy(T["ob%d" % i][:], T["po%d" % i][:, 0:W]).then_inc(sem["cp%d" % i], 1)
+    acc = T.po0
+    for t, j in enumerate(after):
+        g.vector.wait_ge(sem["oa%d" % j], ne)
+        if t > 0:
+            g.vector.wait_ge(sem.ad, t)
+        if t == n - 2:
+            out = T.ybuf[:]
+            nxt = None
+        else:
+            nxt = T.pacc if t % 2 == 0 else T.po0
+            out = nxt[:, 0:W]
+        g.vector.tensor_tensor(out, acc[:, 0:W], T["ol%d" % j][:], AluOpType.add).then_inc(sem.ad, 1)
+        acc = nxt
+
+    g.sync.wait_ge(sem.ad, n - 1)
+    g.sync.dma_start(T.y[:], T.ybuf[:]).then_inc(sem.st, 16)
+    g.sync.wait_ge(sem.st, 16)

@@ -13,14 +13,17 @@ SCRATCH = {
     "ps1": ("psum", [128, 512], "float32"),
     "pacc": ("psum", [128, 512], "float32"),
 }
-SEMAPHORES = ["qld", "kld", "vld", "zf", "sm", "rl", "om", "ad", "sent", "st"]
+SEMAPHORES = ["qld", "kld", "vld", "zf", "ad", "sent", "st"]
 for _j in range(N):
     SCRATCH["ql%d" % _j] = ("sbuf", [128, W], "bfloat16")
     SCRATCH["ol%d" % _j] = ("sbuf", [128, W], "bfloat16")
     SCRATCH["sb%d" % _j] = ("sbuf", [128, W], "bfloat16")
     SCRATCH["ob%d" % _j] = ("sbuf", [128, W], "bfloat16")
     SCRATCH["po%d" % _j] = ("psum", [128, 512], "float32")
-    SEMAPHORES += ["qa%d" % _j, "oa%d" % _j, "cp%d" % _j]
+    SEMAPHORES += ["qa%d" % _j, "oa%d" % _j, "cp%d" % _j, "sm%d" % _j, "rl%d" % _j, "om%d" % _j]
+
+T_ORDER = [("S", 0), ("O", 0), ("S", 1), ("S", 2), ("O", 1), ("S", 3), ("O", 2), ("S", 4), ("O", 3), ("O", 4)]
+V_ORDER = [("R", 0), ("R", 1), ("R", 2), ("C", 1), ("R", 3), ("C", 2), ("R", 4), ("C", 3), ("C", 4)]
 
 
 def rank_program(g, core, T, topo):
@@ -39,8 +42,7 @@ def rank_program(g, core, T, topo):
 
     g.sync.dma_start(myq[:], T.q[:]).then_inc(sem.qld, 16)
     g.sync.dma_start(T.ks[:], T.k[:]).then_inc(sem.kld, 16)
-    g.scalar.wait_ge(sem.qld, 16)
-    g.scalar.dma_start(T.vs[:], T.v[:]).then_inc(sem.vld, 16)
+    g.sync.dma_start(T.vs[:], T.v[:]).then_inc(sem.vld, 16)
     g.vector.memset(T.zero[:], 0.0).then_inc(sem.zf, 1)
 
     g.wait_ge(sem.qld, 16)
@@ -59,7 +61,8 @@ def rank_program(g, core, T, topo):
         g.remote_dma(T["ol%d" % r][:], T["ob%d" % i][:], sem["oa%d" % r], sem.sent, pid, rid, mask)
     g.wait_ge(sem.sent, ne * n)
 
-    for i, j in enumerate(items):
+    def op_s(i):
+        j = items[i]
         if i == 0:
             g.tensor.wait_ge(sem.qld, 16)
             g.tensor.wait_ge(sem.kld, 16)
@@ -68,23 +71,32 @@ def rank_program(g, core, T, topo):
         ps, qj = T["ps%d" % (i % 2)], T["ql%d" % j]
         for h in range(NH):
             g.tensor.matmul(ps[:, h * QP:(h + 1) * QP], T.ks[:, h * KP:(h + 1) * KP],
-                            qj[:, h * QP:(h + 1) * QP], True, True).then_inc(sem.sm, 1)
+                            qj[:, h * QP:(h + 1) * QP], True, True).then_inc(sem["sm%d" % i], 1)
+
+    def op_o(i):
         if i == 0:
             g.tensor.wait_ge(sem.vld, 16)
-        g.tensor.wait_ge(sem.rl, i + 1)
+        g.tensor.wait_ge(sem["rl%d" % i], 1)
         po, sb = T["po%d" % i], T["sb%d" % i]
         for h in range(NH):
             g.tensor.matmul(po[:, h * QP:(h + 1) * QP], T.vs[:, h * KP:(h + 1) * KP],
-                            sb[:, h * QP:(h + 1) * QP], True, True).then_inc(sem.om, 1)
+                            sb[:, h * QP:(h + 1) * QP], True, True).then_inc(sem["om%d" % i], 1)
+
+    def op_r(i):
+        g.vector.wait_ge(sem["sm%d" % i], NH)
+        g.vector.tensor_tensor(T["sb%d" % i][:], T["ps%d" % (i % 2)][:, 0:W], T.zero[:],
+                               AluOpType.max).then_inc(sem["rl%d" % i], 1)
+
+    def op_c(i):
+        g.vector.wait_ge(sem["om%d" % i], NH)
+        g.vector.tensor_copy(T["ob%d" % i][:], T["po%d" % i][:, 0:W]).then_inc(sem["cp%d" % i], 1)
 
     g.vector.wait_ge(sem.zf, 1)
-    for i in range(n):
-        g.vector.wait_ge(sem.sm, NH * (i + 1))
-        g.vector.tensor_tensor(T["sb%d" % i][:], T["ps%d" % (i % 2)][:, 0:W], T.zero[:],
-                               AluOpType.max).then_inc(sem.rl, 1)
-        if i > 0:
-            g.vector.wait_ge(sem.om, NH * (i + 1))
-            g.vector.tensor_copy(T["ob%d" % i][:], T["po%d" % i][:, 0:W]).then_inc(sem["cp%d" % i], 1)
+    for kind, i in T_ORDER:
+        (op_s if kind == "S" else op_o)(i)
+    for kind, i in V_ORDER:
+        (op_r if kind == "R" else op_c)(i)
+    g.vector.wait_ge(sem.om0, NH)
     acc = T.po0
     for t, j in enumerate(after):
         g.vector.wait_ge(sem["oa%d" % j], ne)

from concourse.bass import DstId, RemoteDMATransfer
from concourse.mybir import AluOpType

N, NH, QP, KP = 5, 5, 32, 128
W = NH * QP

SCRATCH = {
    "ks": ("sbuf", [128, NH * KP], "bfloat16"),
    "vs": ("sbuf", [128, NH * KP], "bfloat16"),
    "zero": ("sbuf", [128, W], "float32"),
    "ybuf": ("sbuf", [128, W], "bfloat16"),
    "ps0": ("psum", [128, 512], "float32"),
    "ps1": ("psum", [128, 512], "float32"),
    "pacc": ("psum", [128, 512], "float32"),
}
SEMAPHORES = ["qld", "kld", "vld", "zf", "ad", "sent", "st"]
for _j in range(N):
    SCRATCH["ql%d" % _j] = ("sbuf", [128, W], "bfloat16")
    SCRATCH["ol%d" % _j] = ("sbuf", [128, W], "bfloat16")
    SCRATCH["sb%d" % _j] = ("sbuf", [128, W], "bfloat16")
    SCRATCH["ob%d" % _j] = ("sbuf", [128, W], "bfloat16")
    SCRATCH["po%d" % _j] = ("psum", [128, 512], "float32")
    SEMAPHORES += ["qa%d" % _j, "oa%d" % _j, "cp%d" % _j, "sm%d" % _j, "rl%d" % _j, "om%d" % _j]

T_ORDER = [("S", 0), ("O", 0), ("S", 1), ("S", 2), ("O", 1), ("S", 3), ("O", 2), ("S", 4), ("O", 3), ("O", 4)]
V_ORDER = [("R", 0), ("R", 1), ("R", 2), ("C", 1), ("R", 3), ("C", 2), ("R", 4), ("C", 3), ("C", 4)]


def rank_program(g, core, T, topo):
    r = T.rank_of(core)
    if r is None:
        return
    cores, sem = T.cores, T.sem
    n = len(cores)
    after = [(r + d) % n for d in range(1, n)]
    items = [r] + [(r - d) % n for d in range(1, n)]
    mask = topo.mask(core, cores[after[0]])
    for j in after:
        mask &= topo.mask(core, cores[j])
    ne = bin(mask).count("1")
    myq = T["ql%d" % r]

    g.sync.dma_start(myq[:], T.q[:]).then_inc(sem.qld, 16)
    g.sync.dma_start(T.ks[:], T.k[:]).then_inc(sem.kld, 16)
    g.sync.dma_start(T.vs[:], T.v[:]).then_inc(sem.vld, 16)
    g.vector.memset(T.zero[:], 0.0).then_inc(sem.zf, 1)

    g.wait_ge(sem.qld, 16)
    ids = []
    for j in after:
        rid, pid, _se = topo.addr(cores[j])
        ids.append(DstId(rid=rid, pnc=pid))
    g.remote_dma_fused(
        [RemoteDMATransfer(dst_ids=ids, dma_engine_mask=mask, remote_sem=sem["qa%d" % r],
                           srcs=[myq[:]], dsts=[myq[:] for _ in after], alu_op=0)],
        local_sem=sem.sent)
    for i in range(1, n):
        j = items[i]
        rid, pid, _se = topo.addr(cores[j])
        g.wait_ge(sem["cp%d" % i], 1)
        g.remote_dma(T["ol%d" % r][:], T["ob%d" % i][:], sem["oa%d" % r], sem.sent, pid, rid, mask)
    g.wait_ge(sem.sent, ne * n)

    def op_s(i):
        j = items[i]
        if i == 0:
            g.tensor.wait_ge(sem.qld, 16)
            g.tensor.wait_ge(sem.kld, 16)
        else:
            g.tensor.wait_ge(sem["qa%d" % j], ne)
        ps, qj = T["ps%d" % (i % 2)], T["ql%d" % j]
        for h in range(NH):
            g.tensor.matmul(ps[:, h * QP:(h + 1) * QP], T.ks[:, h * KP:(h + 1) * KP],
                            qj[:, h * QP:(h + 1) * QP], True, True).then_inc(sem["sm%d" % i], 1)

    def op_o(i):
        if i == 0:
            g.tensor.wait_ge(sem.vld, 16)
        g.tensor.wait_ge(sem["rl%d" % i], 1)
        po, sb = T["po%d" % i], T["sb%d" % i]
        for h in range(NH):
            g.tensor.matmul(po[:, h * QP:(h + 1) * QP], T.vs[:, h * KP:(h + 1) * KP],
                            sb[:, h * QP:(h + 1) * QP], True, True).then_inc(sem["om%d" % i], 1)

    def op_r(i):
        g.vector.wait_ge(sem["sm%d" % i], NH)
        g.vector.tensor_tensor(T["sb%d" % i][:], T["ps%d" % (i % 2)][:, 0:W], T.zero[:],
                               AluOpType.max).then_inc(sem["rl%d" % i], 1)

    def op_c(i):
        g.vector.wait_ge(sem["om%d" % i], NH)
        g.vector.tensor_copy(T["ob%d" % i][:], T["po%d" % i][:, 0:W]).then_inc(sem["cp%d" % i], 1)

    g.vector.wait_ge(sem.zf, 1)
    for kind, i in T_ORDER:
        (op_s if kind == "S" else op_o)(i)
    for kind, i in V_ORDER:
        (op_r if kind == "R" else op_c)(i)
    g.vector.wait_ge(sem.om0, NH)
    acc = T.po0
    for t, j in enumerate(after):
        g.vector.wait_ge(sem["oa%d" % j], ne)
        if t > 0:
            g.vector.wait_ge(sem.ad, t)
        if t == n - 2:
            out = T.ybuf[:]
            nxt = None
        else:
            nxt = T.pacc if t % 2 == 0 else T.po0
            out = nxt[:, 0:W]
        g.vector.tensor_tensor(out, acc[:, 0:W], T["ol%d" % j][:], AluOpType.add).then_inc(sem.ad, 1)
        acc = nxt

    g.sync.wait_ge(sem.ad, n - 1)
    g.sync.dma_start(T.y[:], T.ybuf[:]).then_inc(sem.st, 16)
    g.sync.wait_ge(sem.st, 16)
